import numpy as np
import ml_dtypes


def mxq(x, axis, fmt="e4m3"):
    dtype, down = {"e4m3": (ml_dtypes.float8_e4m3fn, 7), "e5m2": (ml_dtypes.float8_e5m2, 14)}[fmt]
    v = np.moveaxis(np.asarray(x, np.float32).astype(ml_dtypes.bfloat16).astype(np.float64), axis, -1)
    blocks = v.reshape(v.shape[:-1] + (-1, 32))
    amax = np.abs(blocks).max(-1, keepdims=True)
    byte = np.maximum(np.where(amax > 0, np.frexp(amax)[1] - 1 + 127, 0) - down, 1)
    scale = np.exp2(byte - 127.0)
    codes = (blocks / scale).astype(np.float32).astype(dtype).astype(np.float64)
    return np.moveaxis((codes * scale).reshape(v.shape), -1, axis)


WIDE = False


def mx_kscale(k):
    if not WIDE:
        return np.ones(k)
    levels = np.array([10, -10, 5, -5, 0])
    if k % 512:
        return np.exp2(np.random.permutation(np.resize(levels, k // 32))).repeat(32)
    a = np.empty((k // 512, 16))
    for p in range(k // 512):
        a[p, :8] = np.random.permutation(np.resize(levels, 8))
        for g in range(8):
            far = levels[np.abs(levels - a[p, g]) >= 10]
            a[p, g + 8] = far[np.random.randint(len(far))]
    return np.exp2(a.ravel()).repeat(32)


def f64(x):
    return np.asarray(x).astype(np.float64)


def striped(idx):
    return np.tile(idx.reshape(-1, 16).T, (8, 1)).astype(np.uint16)


def unstriped(offs):
    return offs[:16].T.reshape(-1).astype(np.int64)


def pack_weight(w):
    k, n = w.shape
    w = f64(np.asarray(w, np.float32).astype(ml_dtypes.bfloat16)).reshape(k // 32, 32, n)
    amax = np.abs(w).max(1)
    byte = np.clip(np.where(amax > 0, np.frexp(amax)[1] - 1 + 127 - 7, 1), 1, 254)
    scaled = (w * np.exp2(127.0 - byte)[:, None, :]).reshape(k, n).astype(np.float32)
    words = np.ascontiguousarray(scaled.reshape(k // 512, 128, 4, n).transpose(0, 1, 3, 2)).astype(ml_dtypes.float8_e4m3fn).view(np.uint8)
    return words, np.ascontiguousarray(byte.astype(np.uint8).reshape(k // 512, 16, n))


def unpack_weight(words, scales):
    g, p, n, _ = words.shape
    vals = np.ascontiguousarray(words).view(ml_dtypes.float8_e4m3fn).astype(np.float64) * np.repeat(np.exp2(scales.astype(np.float64) - 127.0), 8, axis=1)[..., None]
    return vals.transpose(0, 1, 3, 2).reshape(g * 512, n)


K, T, S, N, H, W = 512, 2048, 512, 256, 512, 1024


def setup_inputs():
    n = np.random.standard_normal
    s = mx_kscale(K)[:, None]
    u = mx_kscale(H)
    packed_xT = pack_weight(n((K, T)) * s)
    packed_eT = pack_weight(n((K, W)) * s)
    return {
        "x_words": packed_xT[0],
        "x_scales": packed_xT[1],
        "w1": (n((K, H)) / np.sqrt(K) / s).astype(np.float32),
        "e_words": packed_eT[0],
        "e_scales": packed_eT[1],
        "w2": (n((K, H)) / np.sqrt(K) / s).astype(np.float32),
        "mag": (np.random.uniform(0.5, 1.6, (H, 1))).astype(np.float32),
        "unit": (np.random.uniform(0.6, 1.4, (H, 1)) * u[:, None]).astype(np.float32),
        "w3": (n((H, N)) / np.sqrt(H) / u[:, None]).astype(np.float32),
        "offs": striped(np.random.permutation(T)[:S]),
        "adp": striped(np.random.permutation(W)[:S]),
        "req": striped(np.random.permutation(S)),
    }


def reference(x_words, x_scales, w1, e_words, e_scales, w2, mag, unit, w3, offs, adp, req):
    xq = unpack_weight(x_words, x_scales)[:, unstriped(offs)]
    y = mxq(f64(w1), 0, "e4m3").T @ xq
    e_adp = unpack_weight(e_words, e_scales)[:, unstriped(adp)]
    ye = mxq(f64(w2), 0, "e4m3").T @ e_adp
    drc = y + 0.7 * ye
    wsq = (drc) ** 2
    msq = wsq.mean(axis=1, keepdims=True)
    nrm = np.sqrt(msq + 0.1)
    out1 = f64(mag) * (drc / nrm)
    yr = y[:, unstriped(req)]
    hid = f64(unit) * (out1 * yr + ye)
    return mxq(f64(w3), 0, "e4m3").T @ mxq(hid, 0, "e4m3")

@@ -1,0 +1,223 @@
+import concourse.mybir as mybir
+
+K, T, S, N, H, W = 512, 2048, 512, 256, 512, 1024
+FLOPS = 2 * S * (K * H + K * H + H * N)
+
+F32 = mybir.dt.float32
+BF16 = mybir.dt.bfloat16
+I32 = mybir.dt.int32
+U32 = mybir.dt.uint32
+U16 = mybir.dt.uint16
+U8 = mybir.dt.uint8
+FP8X4 = mybir.dt.float8_e4m3fn_x4
+ACT = mybir.ActivationFunctionType
+ALU = mybir.AluOpType
+
+P = 128
+PACK = 4
+LINE = 4
+W1_VECTOR_M = 48
+PARTS = (256, 128, 128)
+
+
+def tile_picked_ydorax_req_p_kernel(
+    tc, x_words, x_scales, w1, e_words, e_scales, w2, mag, unit, w3, offs, adp, req, out
+):
+    nc = tc.nc
+    with tc.tile_pool(name="keep", bufs=1) as keep, tc.psum_pool(name="psum", bufs=1) as psum:
+        offs_sb = keep.tile([P, S // 16], U16, name="offs_sb")
+        adp_sb = keep.tile([P, S // 16], U16, name="adp_sb")
+        req_sb = keep.tile([P, S // 16], U16, name="req_sb")
+        x_table = keep.tile([P, T], I32, name="x_table")
+        e_table = keep.tile([P, W], I32, name="e_table")
+        x_scale_table = keep.tile([P, T], U8, name="x_scale_table")
+        e_scale_table = keep.tile([P, W], U8, name="e_scale_table")
+        w1_raw = keep.tile([P, PACK, H], F32, name="w1_raw")
+        w2_raw = keep.tile([P, PACK, H], F32, name="w2_raw")
+        w3_raw = keep.tile([P, PACK, N], F32, name="w3_raw")
+        mag_sb = keep.tile([P, PACK], F32, name="mag_sb")
+        unit_sb = keep.tile([P, PACK], F32, name="unit_sb")
+
+        nc.vector.memset(x_scale_table[:].bitcast(I32), 0)
+        nc.vector.memset(e_scale_table[:].bitcast(I32), 0)
+
+        def load_scale_rows(table, scales):
+            for q in range(4):
+                nc.sync.dma_start(
+                    out=table[32 * q : 32 * q + 4, :].bitcast(I32),
+                    in_=scales[0, 4 * q : 4 * q + 4, :].bitcast(I32),
+                )
+
+        def load_words(table, words):
+            nc.sync.dma_start(out=table[:], in_=words[0].rearrange("p n t -> p (n t)").bitcast(I32))
+
+        def load_rows(raw, weight):
+            nc.sync.dma_start(out=raw[:], in_=weight.rearrange("(p j) c -> p j c", j=PACK))
+
+        nc.sync.dma_start(offs_sb[:], offs)
+        load_rows(w1_raw, w1)
+        load_scale_rows(x_scale_table, x_scales)
+        load_words(x_table, x_words)
+        nc.sync.dma_start(adp_sb[:], adp)
+        load_words(e_table, e_words)
+        load_scale_rows(e_scale_table, e_scales)
+        load_rows(w2_raw, w2)
+        nc.sync.dma_start(req_sb[:], req)
+        load_rows(w3_raw, w3)
+        nc.gpsimd.dma_start(out=mag_sb[:], in_=mag.rearrange("(p t) o -> p (t o)", t=PACK))
+        nc.gpsimd.dma_start(out=unit_sb[:], in_=unit.rearrange("(p t) o -> p (t o)", t=PACK))
+
+        y_rows = [keep.tile([P, S], F32, name=f"y_rows{t}") for t in range(PACK)]
+        minus_half = keep.tile([P, 2], F32, name="minus_half")
+        nc.gpsimd.memset(minus_half[:], -0.5)
+        mag_unit = keep.tile([P, PACK], F32, name="mag_unit")
+        nc.gpsimd.tensor_tensor(out=mag_unit[:], in0=mag_sb[:], in1=unit_sb[:], op=ALU.mult)
+
+        def gather(name, dtype, window, offsets):
+            picked = keep.tile([P, S], dtype, name=name, align_bytes=64)
+            nc.vector.tensor_copy(out=picked[:], in_=window.indirect(offsets[:]))
+            return picked
+
+        def round_dealt(copy, grouped, raw, m0, m1):
+            copy(
+                out=grouped[:, :, m0:m1, :].rearrange("p t m j -> p m j t"),
+                in_=raw[:, :, PACK * m0 : PACK * m1].rearrange("p j (m t) -> p m j t", t=PACK),
+            )
+
+        def quantize(name, values, width):
+            codes = keep.tile([P, width], U32, name=name + "_codes", align_bytes=64)
+            scales = keep.tile([P, width], U8, name=name + "_scales", align_bytes=64)
+            nc.vector.quantize_mx(out=codes[:].bitcast(FP8X4), scales=scales[:], in_=values)
+            return codes, scales
+
+        def product(acc, stationary, moving):
+            nc.tensor.matmul_mx(
+                out=acc,
+                lhsT=stationary[0].bitcast(FP8X4),
+                lhsT_scale=stationary[1],
+                rhs=moving[0].bitcast(FP8X4),
+                rhs_scale=moving[1],
+                start=True,
+                stop=True,
+            )
+
+        x_scale_picked = gather("x_scale_picked", U8, x_scale_table[:], offs_sb)
+        w1_grouped = keep.tile([P, PACK, P, PACK], BF16, name="w1_grouped", align_bytes=64)
+        round_dealt(nc.scalar.copy, w1_grouped, w1_raw, W1_VECTOR_M, P)
+        round_dealt(nc.vector.tensor_copy, w1_grouped, w1_raw, 0, W1_VECTOR_M)
+        w1_q = [quantize(f"w1_{t}", w1_grouped[:, t].rearrange("p m j -> p (m j)"), P) for t in range(PACK)]
+        x_picked = gather("x_picked", U32, x_table[:].bitcast(U32), offs_sb)
+        y_banks = [psum.tile([P, S], F32, name=f"y_bank{t}", tag=f"bank{t}") for t in range(PACK)]
+        for t in range(PACK):
+            product(y_banks[t][:], (w1_q[t][0][:], w1_q[t][1][:]), (x_picked[:], x_scale_picked[:]))
+        y_req = [keep.tile([P, S], F32, name=f"y_req{t}") for t in range(PACK)]
+        for t in range(PACK):
+            nc.scalar.copy(out=y_rows[t][:], in_=y_banks[t][:])
+
+        def fetch(t, on_scalar):
+            for c0 in range(0, S, S // 2):
+                window = y_rows[t][:].indirect(req_sb[:, c0 // 16 : (c0 + S // 2) // 16])
+                if on_scalar:
+                    nc.scalar.activation(out=y_req[t][:, c0 : c0 + S // 2], in_=window, func=ACT.Copy)
+                else:
+                    nc.vector.tensor_copy(out=y_req[t][:, c0 : c0 + S // 2], in_=window)
+
+        fetch(0, True)
+        fetch(1, True)
+
+        e_scale_picked = gather("e_scale_picked", U8, e_scale_table[:], adp_sb)
+        e_picked = gather("e_picked", U32, e_table[:].bitcast(U32), adp_sb)
+        w2_grouped = keep.tile([P, PACK, P, PACK], BF16, name="w2_grouped", align_bytes=64)
+        round_dealt(nc.vector.tensor_copy, w2_grouped, w2_raw, 0, P)
+        w2_q = [quantize(f"w2_{t}", w2_grouped[:, t].rearrange("p m j -> p (m j)"), P) for t in range(PACK)]
+        ye_banks = [psum.tile([P, S], F32, name=f"ye_bank{t}", tag=f"bank{PACK + t}") for t in range(PACK)]
+        for t in range(PACK):
+            product(ye_banks[t][:], (w2_q[t][0][:], w2_q[t][1][:]), (e_picked[:], e_scale_picked[:]))
+
+        w3_grouped = keep.tile([P, N, PACK], BF16, name="w3_grouped", align_bytes=64)
+        nc.vector.tensor_copy(
+            out=w3_grouped[:].rearrange("p (c i) j -> p c j i", i=LINE),
+            in_=w3_raw[:].rearrange("p j (c i) -> p c j i", i=LINE),
+        )
+
+        drc = [keep.tile([P, S], F32, name=f"drc{t}") for t in range(PACK)]
+        factor = [keep.tile([P, 2], F32, name=f"factor{g}") for g in range(PACK // 2)]
+        for g in range(PACK // 2):
+            sum_sq = keep.tile([P, 2], F32, name=f"sum_sq{g}")
+            for u in range(2):
+                t = 2 * g + u
+                nc.vector.scalar_tensor_tensor(
+                    out=drc[t][:], in0=ye_banks[t][:], scalar=0.7, in1=y_rows[t][:], op0=ALU.mult, op1=ALU.add
+                )
+                squares = keep.tile([P, S], BF16, name="squares", bufs=2)
+                nc.scalar.activation(out=squares[:], in_=drc[t][:], func=ACT.Square, accum_out=sum_sq[:, u : u + 1])
+            msq_eps = keep.tile([P, 2], F32, name=f"msq_eps{g}")
+            nc.gpsimd.tensor_scalar(
+                out=msq_eps[:], in0=sum_sq[:], scalar1=1.0 / S, scalar2=0.1, op0=ALU.mult, op1=ALU.add
+            )
+            inv_nrm = keep.tile([P, 2], F32, name=f"inv_nrm{g}")
+            nc.gpsimd.tensor_tensor(out=inv_nrm[:], in0=msq_eps[:], in1=minus_half[:], op=ALU.pow)
+            nc.gpsimd.tensor_tensor(
+                out=factor[g][:], in0=inv_nrm[:], in1=mag_unit[:, 2 * g : 2 * g + 2], op=ALU.mult
+            )
+        fetch(2, False)
+        fetch(3, True)
+
+        w3_q = quantize("w3", w3_grouped[:].rearrange("p n j -> p (n j)"), N)
+
+        gated = keep.tile([P, PACK, S], F32, name="gated")
+        for t in range(PACK):
+            nc.vector.scalar_tensor_tensor(
+                out=gated[:, t, :],
+                in0=y_req[t][:],
+                scalar=factor[t // 2][:, t % 2 : t % 2 + 1],
+                in1=drc[t][:],
+                op0=ALU.mult,
+                op1=ALU.mult,
+            )
+        half = S // 2
+        unit_ye = [keep.tile([P, PACK, half], F32, name=f"unit_ye{g}") for g in range(2)]
+        for g in range(2):
+            for t in range(PACK):
+                nc.scalar.activation(
+                    out=unit_ye[g][:, t, :],
+                    in_=ye_banks[t][:, g * half : (g + 1) * half],
+                    func=ACT.Copy,
+                    scale=unit_sb[:, t : t + 1],
+                )
+
+        starts = [sum(PARTS[:h]) for h in range(len(PARTS))]
+        hid = []
+
+        def combine(h):
+            c0, width = starts[h], PARTS[h]
+            part = keep.tile([P, width, PACK], BF16, name=f"hid{h}", align_bytes=64)
+            nc.vector.tensor_tensor(
+                out=part[:].rearrange("p (c i) t -> p c t i", i=LINE),
+                in0=gated[:, :, c0 : c0 + width].rearrange("p t (c i) -> p c t i", i=LINE),
+                in1=unit_ye[c0 // half][:, :, c0 % half : c0 % half + width].rearrange("p t (c i) -> p c t i", i=LINE),
+                op=ALU.add,
+            )
+            hid.append(part)
+
+        def finish(h):
+            c0, width = starts[h], PARTS[h]
+            last = h == len(PARTS) - 1
+            hid_q = quantize(f"hid{h}", hid[h][:].rearrange("p s t -> p (s t)"), width)
+            for m in range(N // P):
+                rows = slice(m * P, (m + 1) * P)
+                acc = psum.tile([P, width], F32, name=f"out_bank{h}{m}", tag=f"bank{h * (N // P) + m}")
+                product(acc[:], (w3_q[0][:, rows], w3_q[1][:, rows]), (hid_q[0][:], hid_q[1][:]))
+                result = keep.tile([P, width], F32, name=f"result{h}{m}")
+                if last and m == 0:
+                    nc.vector.tensor_copy(out=result[:], in_=acc[:])
+                else:
+                    nc.scalar.copy(out=result[:], in_=acc[:])
+                queue = nc.scalar if last and m == 1 else nc.sync
+                queue.dma_start(out=out[rows, c0 : c0 + width], in_=result[:])
+
+        combine(0)
+        for h in range(1, len(PARTS)):
+            combine(h)
+            finish(h - 1)
+        finish(len(PARTS) - 1)

@@ -16,8 +16,9 @@ ALU = mybir.AluOpType
 P = 128
 PACK = 4
 LINE = 4
-W1_VECTOR_M = 48
-PARTS = (256, 128, 128)
+W1_VECTOR_M = 88
+HALF = S // 2
+PARTS = ((0, 256), (256, 128), (384, 128))
 
 
 def tile_picked_ydorax_req_p_kernel(
@@ -41,9 +42,13 @@ def tile_picked_ydorax_req_p_kernel(
         nc.vector.memset(x_scale_table[:].bitcast(I32), 0)
         nc.vector.memset(e_scale_table[:].bitcast(I32), 0)
 
-        def load_scale_rows(table, scales):
+        warm = keep.tile([P, 2], F32, name="warm")
+        nc.gpsimd.memset(warm[:, 0:1], 1.0)
+        nc.scalar.activation(out=warm[:, 1:2], in_=warm[:, 0:1], func=ACT.Sqrt)
+
+        def load_scale_rows(queue, table, scales):
             for q in range(4):
-                nc.sync.dma_start(
+                queue.dma_start(
                     out=table[32 * q : 32 * q + 4, :].bitcast(I32),
                     in_=scales[0, 4 * q : 4 * q + 4, :].bitcast(I32),
                 )
@@ -55,23 +60,19 @@ def tile_picked_ydorax_req_p_kernel(
             nc.sync.dma_start(out=raw[:], in_=weight.rearrange("(p j) c -> p j c", j=PACK))
 
         nc.sync.dma_start(offs_sb[:], offs)
-        load_rows(w1_raw, w1)
-        load_scale_rows(x_scale_table, x_scales)
         load_words(x_table, x_words)
+        load_scale_rows(nc.sync, x_scale_table, x_scales)
         nc.sync.dma_start(adp_sb[:], adp)
+        load_rows(w1_raw, w1)
+        load_scale_rows(nc.sync, e_scale_table, e_scales)
         load_words(e_table, e_words)
-        load_scale_rows(e_scale_table, e_scales)
         load_rows(w2_raw, w2)
         nc.sync.dma_start(req_sb[:], req)
         load_rows(w3_raw, w3)
-        nc.gpsimd.dma_start(out=mag_sb[:], in_=mag.rearrange("(p t) o -> p (t o)", t=PACK))
-        nc.gpsimd.dma_start(out=unit_sb[:], in_=unit.rearrange("(p t) o -> p (t o)", t=PACK))
+        nc.sync.dma_start(out=mag_sb[:], in_=mag.rearrange("(p t) o -> p (t o)", t=PACK))
+        nc.sync.dma_start(out=unit_sb[:], in_=unit.rearrange("(p t) o -> p (t o)", t=PACK))
 
         y_rows = [keep.tile([P, S], F32, name=f"y_rows{t}") for t in range(PACK)]
-        minus_half = keep.tile([P, 2], F32, name="minus_half")
-        nc.gpsimd.memset(minus_half[:], -0.5)
-        mag_unit = keep.tile([P, PACK], F32, name="mag_unit")
-        nc.gpsimd.tensor_tensor(out=mag_unit[:], in0=mag_sb[:], in1=unit_sb[:], op=ALU.mult)
 
         def gather(name, dtype, window, offsets):
             picked = keep.tile([P, S], dtype, name=name, align_bytes=64)
@@ -101,29 +102,25 @@ def tile_picked_ydorax_req_p_kernel(
                 stop=True,
             )
 
+        x_picked = gather("x_picked", U32, x_table[:].bitcast(U32), offs_sb)
         x_scale_picked = gather("x_scale_picked", U8, x_scale_table[:], offs_sb)
         w1_grouped = keep.tile([P, PACK, P, PACK], BF16, name="w1_grouped", align_bytes=64)
         round_dealt(nc.scalar.copy, w1_grouped, w1_raw, W1_VECTOR_M, P)
         round_dealt(nc.vector.tensor_copy, w1_grouped, w1_raw, 0, W1_VECTOR_M)
         w1_q = [quantize(f"w1_{t}", w1_grouped[:, t].rearrange("p m j -> p (m j)"), P) for t in range(PACK)]
-        x_picked = gather("x_picked", U32, x_table[:].bitcast(U32), offs_sb)
         y_banks = [psum.tile([P, S], F32, name=f"y_bank{t}", tag=f"bank{t}") for t in range(PACK)]
         for t in range(PACK):
             product(y_banks[t][:], (w1_q[t][0][:], w1_q[t][1][:]), (x_picked[:], x_scale_picked[:]))
-        y_req = [keep.tile([P, S], F32, name=f"y_req{t}") for t in range(PACK)]
         for t in range(PACK):
             nc.scalar.copy(out=y_rows[t][:], in_=y_banks[t][:])
 
-        def fetch(t, on_scalar):
-            for c0 in range(0, S, S // 2):
-                window = y_rows[t][:].indirect(req_sb[:, c0 // 16 : (c0 + S // 2) // 16])
-                if on_scalar:
-                    nc.scalar.activation(out=y_req[t][:, c0 : c0 + S // 2], in_=window, func=ACT.Copy)
-                else:
-                    nc.vector.tensor_copy(out=y_req[t][:, c0 : c0 + S // 2], in_=window)
+        def fetch(target, t, g):
+            window = y_rows[t][:].indirect(req_sb[:, g * HALF // 16 : (g + 1) * HALF // 16])
+            nc.scalar.activation(out=target[:, t, :], in_=window, func=ACT.Copy)
 
-        fetch(0, True)
-        fetch(1, True)
+        y_req = [keep.tile([P, PACK, HALF], F32, name="y_req0")]
+        for t in range(PACK):
+            fetch(y_req[0], t, 0)
 
         e_scale_picked = gather("e_scale_picked", U8, e_scale_table[:], adp_sb)
         e_picked = gather("e_picked", U32, e_table[:].bitcast(U32), adp_sb)
@@ -140,6 +137,8 @@ def tile_picked_ydorax_req_p_kernel(
             in_=w3_raw[:].rearrange("p j (c i) -> p c j i", i=LINE),
         )
 
+        mag_unit = keep.tile([P, PACK], F32, name="mag_unit")
+        nc.vector.tensor_tensor(out=mag_unit[:], in0=mag_sb[:], in1=unit_sb[:], op=ALU.mult)
         drc = [keep.tile([P, S], F32, name=f"drc{t}") for t in range(PACK)]
         factor = [keep.tile([P, 2], F32, name=f"factor{g}") for g in range(PACK // 2)]
         for g in range(PACK // 2):
@@ -149,64 +148,62 @@ def tile_picked_ydorax_req_p_kernel(
                 nc.vector.scalar_tensor_tensor(
                     out=drc[t][:], in0=ye_banks[t][:], scalar=0.7, in1=y_rows[t][:], op0=ALU.mult, op1=ALU.add
                 )
-                squares = keep.tile([P, S], BF16, name="squares", bufs=2)
+                squares = keep.tile([P, S], F32, name="squares", tag=f"squares{t}")
                 nc.scalar.activation(out=squares[:], in_=drc[t][:], func=ACT.Square, accum_out=sum_sq[:, u : u + 1])
-            msq_eps = keep.tile([P, 2], F32, name=f"msq_eps{g}")
-            nc.gpsimd.tensor_scalar(
-                out=msq_eps[:], in0=sum_sq[:], scalar1=1.0 / S, scalar2=0.1, op0=ALU.mult, op1=ALU.add
-            )
+            nrm = keep.tile([P, 2], F32, name=f"nrm{g}")
+            nc.scalar.activation(out=nrm[:], in_=sum_sq[:], func=ACT.Sqrt, scale=1.0 / S, bias=0.1)
             inv_nrm = keep.tile([P, 2], F32, name=f"inv_nrm{g}")
-            nc.gpsimd.tensor_tensor(out=inv_nrm[:], in0=msq_eps[:], in1=minus_half[:], op=ALU.pow)
-            nc.gpsimd.tensor_tensor(
+            nc.vector.reciprocal(out=inv_nrm[:], in_=nrm[:])
+            nc.vector.tensor_tensor(
                 out=factor[g][:], in0=inv_nrm[:], in1=mag_unit[:, 2 * g : 2 * g + 2], op=ALU.mult
             )
-        fetch(2, False)
-        fetch(3, True)
 
         w3_q = quantize("w3", w3_grouped[:].rearrange("p n j -> p (n j)"), N)
 
-        gated = keep.tile([P, PACK, S], F32, name="gated")
-        for t in range(PACK):
-            nc.vector.scalar_tensor_tensor(
-                out=gated[:, t, :],
-                in0=y_req[t][:],
-                scalar=factor[t // 2][:, t % 2 : t % 2 + 1],
-                in1=drc[t][:],
-                op0=ALU.mult,
-                op1=ALU.mult,
-            )
-        half = S // 2
-        unit_ye = [keep.tile([P, PACK, half], F32, name=f"unit_ye{g}") for g in range(2)]
-        for g in range(2):
+        unit_ye = [keep.tile([P, PACK, HALF], F32, name=f"unit_ye{g}") for g in range(2)]
+        gated = [keep.tile([P, PACK, HALF], F32, name=f"gated{g}") for g in range(2)]
+
+        def scale_ye(g):
             for t in range(PACK):
                 nc.scalar.activation(
                     out=unit_ye[g][:, t, :],
-                    in_=ye_banks[t][:, g * half : (g + 1) * half],
+                    in_=ye_banks[t][:, g * HALF : (g + 1) * HALF],
                     func=ACT.Copy,
                     scale=unit_sb[:, t : t + 1],
                 )
 
-        starts = [sum(PARTS[:h]) for h in range(len(PARTS))]
+        def gate(g):
+            for t in range(PACK):
+                nc.vector.scalar_tensor_tensor(
+                    out=gated[g][:, t, :],
+                    in0=y_req[g][:, t, :],
+                    scalar=factor[t // 2][:, t % 2 : t % 2 + 1],
+                    in1=drc[t][:, g * HALF : (g + 1) * HALF],
+                    op0=ALU.mult,
+                    op1=ALU.mult,
+                )
+
         hid = []
 
         def combine(h):
-            c0, width = starts[h], PARTS[h]
+            c0, width = PARTS[h]
+            g, local = divmod(c0, HALF)
             part = keep.tile([P, width, PACK], BF16, name=f"hid{h}", align_bytes=64)
             nc.vector.tensor_tensor(
                 out=part[:].rearrange("p (c i) t -> p c t i", i=LINE),
-                in0=gated[:, :, c0 : c0 + width].rearrange("p t (c i) -> p c t i", i=LINE),
-                in1=unit_ye[c0 // half][:, :, c0 % half : c0 % half + width].rearrange("p t (c i) -> p c t i", i=LINE),
+                in0=gated[g][:, :, local : local + width].rearrange("p t (c i) -> p c t i", i=LINE),
+                in1=unit_ye[g][:, :, local : local + width].rearrange("p t (c i) -> p c t i", i=LINE),
                 op=ALU.add,
             )
             hid.append(part)
 
         def finish(h):
-            c0, width = starts[h], PARTS[h]
+            c0, width = PARTS[h]
             last = h == len(PARTS) - 1
             hid_q = quantize(f"hid{h}", hid[h][:].rearrange("p s t -> p (s t)"), width)
             for m in range(N // P):
                 rows = slice(m * P, (m + 1) * P)
-                acc = psum.tile([P, width], F32, name=f"out_bank{h}{m}", tag=f"bank{h * (N // P) + m}")
+                acc = psum.tile([P, width], F32, name=f"out_bank{h}{m}", tag=f"bank{(h * (N // P) + m) % PACK}")
                 product(acc[:], (w3_q[0][:, rows], w3_q[1][:, rows]), (hid_q[0][:], hid_q[1][:]))
                 result = keep.tile([P, width], F32, name=f"result{h}{m}")
                 if last and m == 0:
@@ -216,8 +213,16 @@ def tile_picked_ydorax_req_p_kernel(
                 queue = nc.scalar if last and m == 1 else nc.sync
                 queue.dma_start(out=out[rows, c0 : c0 + width], in_=result[:])
 
+        scale_ye(0)
+        y_req.append(keep.tile([P, PACK, HALF], F32, name="y_req1", tag=f"squares{PACK - 1}"))
+        for t in range(PACK):
+            fetch(y_req[1], t, 1)
+        scale_ye(1)
+        gate(0)
         combine(0)
-        for h in range(1, len(PARTS)):
-            combine(h)
-            finish(h - 1)
-        finish(len(PARTS) - 1)
+        gate(1)
+        finish(0)
+        combine(1)
+        combine(2)
+        finish(1)
+        finish(2)

@@ -16,7 +16,8 @@ ALU = mybir.AluOpType
 P = 128
 PACK = 4
 LINE = 4
-W1_VECTOR_M = 88
+W1_VECTOR_M = 100
+W2_PIECES = ((0, 96), (96, 128))
 HALF = S // 2
 PARTS = ((0, 256), (256, 128), (384, 128))
 
@@ -34,7 +35,9 @@ def tile_picked_ydorax_req_p_kernel(
         x_scale_table = keep.tile([P, T], U8, name="x_scale_table")
         e_scale_table = keep.tile([P, W], U8, name="e_scale_table")
         w1_raw = keep.tile([P, PACK, H], F32, name="w1_raw")
-        w2_raw = keep.tile([P, PACK, H], F32, name="w2_raw")
+        w2_raw = [
+            keep.tile([P, PACK, PACK * (m1 - m0)], F32, name=f"w2_raw{m0}") for m0, m1 in W2_PIECES
+        ]
         w3_raw = keep.tile([P, PACK, N], F32, name="w3_raw")
         mag_sb = keep.tile([P, PACK], F32, name="mag_sb")
         unit_sb = keep.tile([P, PACK], F32, name="unit_sb")
@@ -59,15 +62,16 @@ def tile_picked_ydorax_req_p_kernel(
         def load_rows(raw, weight):
             nc.sync.dma_start(out=raw[:], in_=weight.rearrange("(p j) c -> p j c", j=PACK))
 
-        nc.sync.dma_start(offs_sb[:], offs)
-        load_words(x_table, x_words)
-        load_scale_rows(nc.sync, x_scale_table, x_scales)
-        nc.sync.dma_start(adp_sb[:], adp)
         load_rows(w1_raw, w1)
+        nc.sync.dma_start(offs_sb[:], offs)
+        load_scale_rows(nc.sync, x_scale_table, x_scales)
+        load_words(x_table, x_words)
+        nc.sync.dma_start(adp_sb[:], adp)
+        nc.sync.dma_start(req_sb[:], req)
         load_scale_rows(nc.sync, e_scale_table, e_scales)
         load_words(e_table, e_words)
-        load_rows(w2_raw, w2)
-        nc.sync.dma_start(req_sb[:], req)
+        for raw, (m0, m1) in zip(w2_raw, W2_PIECES):
+            load_rows(raw, w2[:, PACK * m0 : PACK * m1])
         load_rows(w3_raw, w3)
         nc.sync.dma_start(out=mag_sb[:], in_=mag.rearrange("(p t) o -> p (t o)", t=PACK))
         nc.sync.dma_start(out=unit_sb[:], in_=unit.rearrange("(p t) o -> p (t o)", t=PACK))
@@ -75,14 +79,14 @@ def tile_picked_ydorax_req_p_kernel(
         y_rows = [keep.tile([P, S], F32, name=f"y_rows{t}") for t in range(PACK)]
 
         def gather(name, dtype, window, offsets):
-            picked = keep.tile([P, S], dtype, name=name, align_bytes=64)
-            nc.vector.tensor_copy(out=picked[:], in_=window.indirect(offsets[:]))
+            picked = keep.tile([P, 16 * offsets.shape[1]], dtype, name=name, align_bytes=64)
+            nc.vector.tensor_copy(out=picked[:], in_=window.indirect(offsets))
             return picked
 
         def round_dealt(copy, grouped, raw, m0, m1):
             copy(
                 out=grouped[:, :, m0:m1, :].rearrange("p t m j -> p m j t"),
-                in_=raw[:, :, PACK * m0 : PACK * m1].rearrange("p j (m t) -> p m j t", t=PACK),
+                in_=raw.rearrange("p j (m t) -> p m j t", t=PACK),
             )
 
         def quantize(name, values, width):
@@ -102,17 +106,20 @@ def tile_picked_ydorax_req_p_kernel(
                 stop=True,
             )
 
-        x_picked = gather("x_picked", U32, x_table[:].bitcast(U32), offs_sb)
-        x_scale_picked = gather("x_scale_picked", U8, x_scale_table[:], offs_sb)
         w1_grouped = keep.tile([P, PACK, P, PACK], BF16, name="w1_grouped", align_bytes=64)
-        round_dealt(nc.scalar.copy, w1_grouped, w1_raw, W1_VECTOR_M, P)
-        round_dealt(nc.vector.tensor_copy, w1_grouped, w1_raw, 0, W1_VECTOR_M)
-        w1_q = [quantize(f"w1_{t}", w1_grouped[:, t].rearrange("p m j -> p (m j)"), P) for t in range(PACK)]
-        y_banks = [psum.tile([P, S], F32, name=f"y_bank{t}", tag=f"bank{t}") for t in range(PACK)]
-        for t in range(PACK):
-            product(y_banks[t][:], (w1_q[t][0][:], w1_q[t][1][:]), (x_picked[:], x_scale_picked[:]))
-        for t in range(PACK):
-            nc.scalar.copy(out=y_rows[t][:], in_=y_banks[t][:])
+        round_dealt(nc.scalar.copy, w1_grouped, w1_raw[:, :, PACK * W1_VECTOR_M :], W1_VECTOR_M, P)
+        round_dealt(nc.vector.tensor_copy, w1_grouped, w1_raw[:, :, : PACK * W1_VECTOR_M], 0, W1_VECTOR_M)
+        w1_q = quantize("w1", w1_grouped[:].rearrange("p t m j -> p (t m j)"), H)
+        x_scale_picked = gather("x_scale_picked", U8, x_scale_table[:], offs_sb[:])
+        for g in range(2):
+            cols = slice(g * HALF, (g + 1) * HALF)
+            entries = offs_sb[:, g * HALF // 16 : (g + 1) * HALF // 16]
+            x_picked = gather(f"x_picked{g}", U32, x_table[:].bitcast(U32), entries)
+            for t in range(PACK):
+                y_bank = psum.tile([P, HALF], F32, name=f"y_bank{g}{t}", tag=f"bank{PACK * g + t}")
+                dealt = slice(t * P, (t + 1) * P)
+                product(y_bank[:], (w1_q[0][:, dealt], w1_q[1][:, dealt]), (x_picked[:], x_scale_picked[:, cols]))
+                nc.scalar.copy(out=y_rows[t][:, cols], in_=y_bank[:])
 
         def fetch(target, t, g):
             window = y_rows[t][:].indirect(req_sb[:, g * HALF // 16 : (g + 1) * HALF // 16])
@@ -122,10 +129,11 @@ def tile_picked_ydorax_req_p_kernel(
         for t in range(PACK):
             fetch(y_req[0], t, 0)
 
-        e_scale_picked = gather("e_scale_picked", U8, e_scale_table[:], adp_sb)
-        e_picked = gather("e_picked", U32, e_table[:].bitcast(U32), adp_sb)
+        e_scale_picked = gather("e_scale_picked", U8, e_scale_table[:], adp_sb[:])
+        e_picked = gather("e_picked", U32, e_table[:].bitcast(U32), adp_sb[:])
         w2_grouped = keep.tile([P, PACK, P, PACK], BF16, name="w2_grouped", align_bytes=64)
-        round_dealt(nc.vector.tensor_copy, w2_grouped, w2_raw, 0, P)
+        for raw, (m0, m1) in zip(w2_raw, W2_PIECES):
+            round_dealt(nc.vector.tensor_copy, w2_grouped, raw[:], m0, m1)
         w2_q = [quantize(f"w2_{t}", w2_grouped[:, t].rearrange("p m j -> p (m j)"), P) for t in range(PACK)]
         ye_banks = [psum.tile([P, S], F32, name=f"ye_bank{t}", tag=f"bank{PACK + t}") for t in range(PACK)]
         for t in range(PACK):
@@ -149,7 +157,20 @@ def tile_picked_ydorax_req_p_kernel(
                     out=drc[t][:], in0=ye_banks[t][:], scalar=0.7, in1=y_rows[t][:], op0=ALU.mult, op1=ALU.add
                 )
                 squares = keep.tile([P, S], F32, name="squares", tag=f"squares{t}")
-                nc.scalar.activation(out=squares[:], in_=drc[t][:], func=ACT.Square, accum_out=sum_sq[:, u : u + 1])
+                if t < PACK - 1:
+                    nc.scalar.activation(
+                        out=squares[:], in_=drc[t][:], func=ACT.Square, accum_out=sum_sq[:, u : u + 1]
+                    )
+                else:
+                    nc.vector.scalar_tensor_tensor(
+                        out=squares[:],
+                        in0=drc[t][:],
+                        scalar=1.0,
+                        in1=drc[t][:],
+                        op0=ALU.mult,
+                        op1=ALU.mult,
+                        accum_out=sum_sq[:, u : u + 1],
+                    )
             nrm = keep.tile([P, 2], F32, name=f"nrm{g}")
             nc.scalar.activation(out=nrm[:], in_=sum_sq[:], func=ACT.Sqrt, scale=1.0 / S, bias=0.1)
             inv_nrm = keep.tile([P, 2], F32, name=f"inv_nrm{g}")
@@ -199,22 +220,28 @@ def tile_picked_ydorax_req_p_kernel(
 
         def finish(h):
             c0, width = PARTS[h]
-            last = h == len(PARTS) - 1
             hid_q = quantize(f"hid{h}", hid[h][:].rearrange("p s t -> p (s t)"), width)
+            acc = psum.tile([P, N // P, width], F32, name=f"out_bank{h}", tag=f"bank{h}")
             for m in range(N // P):
                 rows = slice(m * P, (m + 1) * P)
-                acc = psum.tile([P, width], F32, name=f"out_bank{h}{m}", tag=f"bank{(h * (N // P) + m) % PACK}")
+                product(acc[:, m, :], (w3_q[0][:, rows], w3_q[1][:, rows]), (hid_q[0][:], hid_q[1][:]))
+            result = keep.tile([P, N // P, width], F32, name=f"result{h}")
+            nc.scalar.copy(out=result[:], in_=acc[:])
+            nc.sync.dma_start(out=out[:, c0 : c0 + width].rearrange("(m p) c -> p m c", p=P), in_=result[:])
+
+        def finish_last(h):
+            c0, width = PARTS[h]
+            hid_q = quantize(f"hid{h}", hid[h][:].rearrange("p s t -> p (s t)"), width)
+            for m, (copy, queue) in enumerate(((nc.vector.tensor_copy, nc.sync), (nc.scalar.copy, nc.scalar))):
+                rows = slice(m * P, (m + 1) * P)
+                acc = psum.tile([P, width], F32, name=f"out_bank{h}{m}", tag=f"bank{h + m}")
                 product(acc[:], (w3_q[0][:, rows], w3_q[1][:, rows]), (hid_q[0][:], hid_q[1][:]))
                 result = keep.tile([P, width], F32, name=f"result{h}{m}")
-                if last and m == 0:
-                    nc.vector.tensor_copy(out=result[:], in_=acc[:])
-                else:
-                    nc.scalar.copy(out=result[:], in_=acc[:])
-                queue = nc.scalar if last and m == 1 else nc.sync
+                copy(out=result[:], in_=acc[:])
                 queue.dma_start(out=out[rows, c0 : c0 + width], in_=result[:])
 
         scale_ye(0)
-        y_req.append(keep.tile([P, PACK, HALF], F32, name="y_req1", tag=f"squares{PACK - 1}"))
+        y_req.append(keep.tile([P, PACK, HALF], F32, name="y_req1", tag=f"squares{PACK - 2}"))
         for t in range(PACK):
             fetch(y_req[1], t, 1)
         scale_ye(1)
@@ -225,4 +252,4 @@ def tile_picked_ydorax_req_p_kernel(
         combine(1)
         combine(2)
         finish(1)
-        finish(2)
+        finish_last(2)

@@ -16,7 +16,7 @@ ALU = mybir.AluOpType
 P = 128
 PACK = 4
 LINE = 4
-W1_VECTOR_M = 100
+W1_VECTOR_M = 84
 W2_PIECES = ((0, 96), (96, 128))
 HALF = S // 2
 PARTS = ((0, 256), (256, 128), (384, 128))
@@ -134,10 +134,14 @@ def tile_picked_ydorax_req_p_kernel(
         w2_grouped = keep.tile([P, PACK, P, PACK], BF16, name="w2_grouped", align_bytes=64)
         for raw, (m0, m1) in zip(w2_raw, W2_PIECES):
             round_dealt(nc.vector.tensor_copy, w2_grouped, raw[:], m0, m1)
-        w2_q = [quantize(f"w2_{t}", w2_grouped[:, t].rearrange("p m j -> p (m j)"), P) for t in range(PACK)]
+        w2_first = quantize("w2_first", w2_grouped[:, 0].rearrange("p m j -> p (m j)"), P)
+        w2_rest = quantize("w2_rest", w2_grouped[:, 1:].rearrange("p t m j -> p (t m j)"), H - P)
+        w2_q = [(w2_first[0][:], w2_first[1][:])] + [
+            (w2_rest[0][:, t * P : (t + 1) * P], w2_rest[1][:, t * P : (t + 1) * P]) for t in range(PACK - 1)
+        ]
         ye_banks = [psum.tile([P, S], F32, name=f"ye_bank{t}", tag=f"bank{PACK + t}") for t in range(PACK)]
         for t in range(PACK):
-            product(ye_banks[t][:], (w2_q[t][0][:], w2_q[t][1][:]), (e_picked[:], e_scale_picked[:]))
+            product(ye_banks[t][:], w2_q[t], (e_picked[:], e_scale_picked[:]))
 
         w3_grouped = keep.tile([P, N, PACK], BF16, name="w3_grouped", align_bytes=64)
         nc.vector.tensor_copy(

import concourse.mybir as mybir

K, T, S, N, H, W = 512, 2048, 512, 256, 512, 1024
FLOPS = 2 * S * (K * H + K * H + H * N)

F32 = mybir.dt.float32
BF16 = mybir.dt.bfloat16
I32 = mybir.dt.int32
U32 = mybir.dt.uint32
U16 = mybir.dt.uint16
U8 = mybir.dt.uint8
FP8X4 = mybir.dt.float8_e4m3fn_x4
ACT = mybir.ActivationFunctionType
ALU = mybir.AluOpType

P = 128
PACK = 4
LINE = 4
W1_VECTOR_M = 84
W2_PIECES = ((0, 96), (96, 128))
HALF = S // 2
PARTS = ((0, 256), (256, 128), (384, 128))


def tile_picked_ydorax_req_p_kernel(
    tc, x_words, x_scales, w1, e_words, e_scales, w2, mag, unit, w3, offs, adp, req, out
):
    nc = tc.nc
    with tc.tile_pool(name="keep", bufs=1) as keep, tc.psum_pool(name="psum", bufs=1) as psum:
        offs_sb = keep.tile([P, S // 16], U16, name="offs_sb")
        adp_sb = keep.tile([P, S // 16], U16, name="adp_sb")
        req_sb = keep.tile([P, S // 16], U16, name="req_sb")
        x_table = keep.tile([P, T], I32, name="x_table")
        e_table = keep.tile([P, W], I32, name="e_table")
        x_scale_table = keep.tile([P, T], U8, name="x_scale_table")
        e_scale_table = keep.tile([P, W], U8, name="e_scale_table")
        w1_raw = keep.tile([P, PACK, H], F32, name="w1_raw")
        w2_raw = [
            keep.tile([P, PACK, PACK * (m1 - m0)], F32, name=f"w2_raw{m0}") for m0, m1 in W2_PIECES
        ]
        w3_raw = keep.tile([P, PACK, N], F32, name="w3_raw")
        mag_sb = keep.tile([P, PACK], F32, name="mag_sb")
        unit_sb = keep.tile([P, PACK], F32, name="unit_sb")

        nc.vector.memset(x_scale_table[:].bitcast(I32), 0)
        nc.vector.memset(e_scale_table[:].bitcast(I32), 0)

        warm = keep.tile([P, 2], F32, name="warm")
        nc.gpsimd.memset(warm[:, 0:1], 1.0)
        nc.scalar.activation(out=warm[:, 1:2], in_=warm[:, 0:1], func=ACT.Sqrt)

        def load_scale_rows(queue, table, scales):
            for q in range(4):
                queue.dma_start(
                    out=table[32 * q : 32 * q + 4, :].bitcast(I32),
                    in_=scales[0, 4 * q : 4 * q + 4, :].bitcast(I32),
                )

        def load_words(table, words):
            nc.sync.dma_start(out=table[:], in_=words[0].rearrange("p n t -> p (n t)").bitcast(I32))

        def load_rows(raw, weight):
            nc.sync.dma_start(out=raw[:], in_=weight.rearrange("(p j) c -> p j c", j=PACK))

        load_rows(w1_raw, w1)
        nc.sync.dma_start(offs_sb[:], offs)
        load_scale_rows(nc.sync, x_scale_table, x_scales)
        load_words(x_table, x_words)
        nc.sync.dma_start(adp_sb[:], adp)
        nc.sync.dma_start(req_sb[:], req)
        load_scale_rows(nc.sync, e_scale_table, e_scales)
        load_words(e_table, e_words)
        for raw, (m0, m1) in zip(w2_raw, W2_PIECES):
            load_rows(raw, w2[:, PACK * m0 : PACK * m1])
        load_rows(w3_raw, w3)
        nc.sync.dma_start(out=mag_sb[:], in_=mag.rearrange("(p t) o -> p (t o)", t=PACK))
        nc.sync.dma_start(out=unit_sb[:], in_=unit.rearrange("(p t) o -> p (t o)", t=PACK))

        y_rows = [keep.tile([P, S], F32, name=f"y_rows{t}") for t in range(PACK)]

        def gather(name, dtype, window, offsets):
            picked = keep.tile([P, 16 * offsets.shape[1]], dtype, name=name, align_bytes=64)
            nc.vector.tensor_copy(out=picked[:], in_=window.indirect(offsets))
            return picked

        def round_dealt(copy, grouped, raw, m0, m1):
            copy(
                out=grouped[:, :, m0:m1, :].rearrange("p t m j -> p m j t"),
                in_=raw.rearrange("p j (m t) -> p m j t", t=PACK),
            )

        def quantize(name, values, width):
            codes = keep.tile([P, width], U32, name=name + "_codes", align_bytes=64)
            scales = keep.tile([P, width], U8, name=name + "_scales", align_bytes=64)
            nc.vector.quantize_mx(out=codes[:].bitcast(FP8X4), scales=scales[:], in_=values)
            return codes, scales

        def product(acc, stationary, moving):
            nc.tensor.matmul_mx(
                out=acc,
                lhsT=stationary[0].bitcast(FP8X4),
                lhsT_scale=stationary[1],
                rhs=moving[0].bitcast(FP8X4),
                rhs_scale=moving[1],
                start=True,
                stop=True,
            )

        w1_grouped = keep.tile([P, PACK, P, PACK], BF16, name="w1_grouped", align_bytes=64)
        round_dealt(nc.scalar.copy, w1_grouped, w1_raw[:, :, PACK * W1_VECTOR_M :], W1_VECTOR_M, P)
        round_dealt(nc.vector.tensor_copy, w1_grouped, w1_raw[:, :, : PACK * W1_VECTOR_M], 0, W1_VECTOR_M)
        w1_q = quantize("w1", w1_grouped[:].rearrange("p t m j -> p (t m j)"), H)
        x_scale_picked = gather("x_scale_picked", U8, x_scale_table[:], offs_sb[:])
        for g in range(2):
            cols = slice(g * HALF, (g + 1) * HALF)
            entries = offs_sb[:, g * HALF // 16 : (g + 1) * HALF // 16]
            x_picked = gather(f"x_picked{g}", U32, x_table[:].bitcast(U32), entries)
            for t in range(PACK):
                y_bank = psum.tile([P, HALF], F32, name=f"y_bank{g}{t}", tag=f"bank{PACK * g + t}")
                dealt = slice(t * P, (t + 1) * P)
                product(y_bank[:], (w1_q[0][:, dealt], w1_q[1][:, dealt]), (x_picked[:], x_scale_picked[:, cols]))
                nc.scalar.copy(out=y_rows[t][:, cols], in_=y_bank[:])

        def fetch(target, t, g):
            window = y_rows[t][:].indirect(req_sb[:, g * HALF // 16 : (g + 1) * HALF // 16])
            nc.scalar.activation(out=target[:, t, :], in_=window, func=ACT.Copy)

        y_req = [keep.tile([P, PACK, HALF], F32, name="y_req0")]
        for t in range(PACK):
            fetch(y_req[0], t, 0)

        e_scale_picked = gather("e_scale_picked", U8, e_scale_table[:], adp_sb[:])
        e_picked = gather("e_picked", U32, e_table[:].bitcast(U32), adp_sb[:])
        w2_grouped = keep.tile([P, PACK, P, PACK], BF16, name="w2_grouped", align_bytes=64)
        for raw, (m0, m1) in zip(w2_raw, W2_PIECES):
            round_dealt(nc.vector.tensor_copy, w2_grouped, raw[:], m0, m1)
        w2_first = quantize("w2_first", w2_grouped[:, 0].rearrange("p m j -> p (m j)"), P)
        w2_rest = quantize("w2_rest", w2_grouped[:, 1:].rearrange("p t m j -> p (t m j)"), H - P)
        w2_q = [(w2_first[0][:], w2_first[1][:])] + [
            (w2_rest[0][:, t * P : (t + 1) * P], w2_rest[1][:, t * P : (t + 1) * P]) for t in range(PACK - 1)
        ]
        ye_banks = [psum.tile([P, S], F32, name=f"ye_bank{t}", tag=f"bank{PACK + t}") for t in range(PACK)]
        for t in range(PACK):
            product(ye_banks[t][:], w2_q[t], (e_picked[:], e_scale_picked[:]))

        w3_grouped = keep.tile([P, N, PACK], BF16, name="w3_grouped", align_bytes=64)
        nc.vector.tensor_copy(
            out=w3_grouped[:].rearrange("p (c i) j -> p c j i", i=LINE),
            in_=w3_raw[:].rearrange("p j (c i) -> p c j i", i=LINE),
        )

        mag_unit = keep.tile([P, PACK], F32, name="mag_unit")
        nc.vector.tensor_tensor(out=mag_unit[:], in0=mag_sb[:], in1=unit_sb[:], op=ALU.mult)
        drc = [keep.tile([P, S], F32, name=f"drc{t}") for t in range(PACK)]
        factor = [keep.tile([P, 2], F32, name=f"factor{g}") for g in range(PACK // 2)]
        for g in range(PACK // 2):
            sum_sq = keep.tile([P, 2], F32, name=f"sum_sq{g}")
            for u in range(2):
                t = 2 * g + u
                nc.vector.scalar_tensor_tensor(
                    out=drc[t][:], in0=ye_banks[t][:], scalar=0.7, in1=y_rows[t][:], op0=ALU.mult, op1=ALU.add
                )
                squares = keep.tile([P, S], F32, name="squares", tag=f"squares{t}")
                if t < PACK - 1:
                    nc.scalar.activation(
                        out=squares[:], in_=drc[t][:], func=ACT.Square, accum_out=sum_sq[:, u : u + 1]
                    )
                else:
                    nc.vector.scalar_tensor_tensor(
                        out=squares[:],
                        in0=drc[t][:],
                        scalar=1.0,
                        in1=drc[t][:],
                        op0=ALU.mult,
                        op1=ALU.mult,
                        accum_out=sum_sq[:, u : u + 1],
                    )
            nrm = keep.tile([P, 2], F32, name=f"nrm{g}")
            nc.scalar.activation(out=nrm[:], in_=sum_sq[:], func=ACT.Sqrt, scale=1.0 / S, bias=0.1)
            inv_nrm = keep.tile([P, 2], F32, name=f"inv_nrm{g}")
            nc.vector.reciprocal(out=inv_nrm[:], in_=nrm[:])
            nc.vector.tensor_tensor(
                out=factor[g][:], in0=inv_nrm[:], in1=mag_unit[:, 2 * g : 2 * g + 2], op=ALU.mult
            )

        w3_q = quantize("w3", w3_grouped[:].rearrange("p n j -> p (n j)"), N)

        unit_ye = [keep.tile([P, PACK, HALF], F32, name=f"unit_ye{g}") for g in range(2)]
        gated = [keep.tile([P, PACK, HALF], F32, name=f"gated{g}") for g in range(2)]

        def scale_ye(g):
            for t in range(PACK):
                nc.scalar.activation(
                    out=unit_ye[g][:, t, :],
                    in_=ye_banks[t][:, g * HALF : (g + 1) * HALF],
                    func=ACT.Copy,
                    scale=unit_sb[:, t : t + 1],
                )

        def gate(g):
            for t in range(PACK):
                nc.vector.scalar_tensor_tensor(
                    out=gated[g][:, t, :],
                    in0=y_req[g][:, t, :],
                    scalar=factor[t // 2][:, t % 2 : t % 2 + 1],
                    in1=drc[t][:, g * HALF : (g + 1) * HALF],
                    op0=ALU.mult,
                    op1=ALU.mult,
                )

        hid = []

        def combine(h):
            c0, width = PARTS[h]
            g, local = divmod(c0, HALF)
            part = keep.tile([P, width, PACK], BF16, name=f"hid{h}", align_bytes=64)
            nc.vector.tensor_tensor(
                out=part[:].rearrange("p (c i) t -> p c t i", i=LINE),
                in0=gated[g][:, :, local : local + width].rearrange("p t (c i) -> p c t i", i=LINE),
                in1=unit_ye[g][:, :, local : local + width].rearrange("p t (c i) -> p c t i", i=LINE),
                op=ALU.add,
            )
            hid.append(part)

        def finish(h):
            c0, width = PARTS[h]
            hid_q = quantize(f"hid{h}", hid[h][:].rearrange("p s t -> p (s t)"), width)
            acc = psum.tile([P, N // P, width], F32, name=f"out_bank{h}", tag=f"bank{h}")
            for m in range(N // P):
                rows = slice(m * P, (m + 1) * P)
                product(acc[:, m, :], (w3_q[0][:, rows], w3_q[1][:, rows]), (hid_q[0][:], hid_q[1][:]))
            result = keep.tile([P, N // P, width], F32, name=f"result{h}")
            nc.scalar.copy(out=result[:], in_=acc[:])
            nc.sync.dma_start(out=out[:, c0 : c0 + width].rearrange("(m p) c -> p m c", p=P), in_=result[:])

        def finish_last(h):
            c0, width = PARTS[h]
            hid_q = quantize(f"hid{h}", hid[h][:].rearrange("p s t -> p (s t)"), width)
            for m, (copy, queue) in enumerate(((nc.vector.tensor_copy, nc.sync), (nc.scalar.copy, nc.scalar))):
                rows = slice(m * P, (m + 1) * P)
                acc = psum.tile([P, width], F32, name=f"out_bank{h}{m}", tag=f"bank{h + m}")
                product(acc[:], (w3_q[0][:, rows], w3_q[1][:, rows]), (hid_q[0][:], hid_q[1][:]))
                result = keep.tile([P, width], F32, name=f"result{h}{m}")
                copy(out=result[:], in_=acc[:])
                queue.dma_start(out=out[rows, c0 : c0 + width], in_=result[:])

        scale_ye(0)
        y_req.append(keep.tile([P, PACK, HALF], F32, name="y_req1", tag=f"squares{PACK - 2}"))
        for t in range(PACK):
            fetch(y_req[1], t, 1)
        scale_ye(1)
        gate(0)
        combine(0)
        gate(1)
        finish(0)
        combine(1)
        combine(2)
        finish(1)
        finish_last(2)
